import numpy as np, ml_dtypes
CORES = [36,38,116,118,124,126,164,166,244,246,252,254]
N = 12
import mx_ref
NC, G = 384, 4
M = NC // N
C = np.float32(0.047)
BF = ml_dtypes.bfloat16
def cut(t, i, w=512):
    return t[:, w * i:w * i + w]
def tile(rs):
    return np.stack(rs, axis=2).reshape(128, -1).astype(BF)
def layer(w, X):
    out = []
    for i in range(G):
        for t in range(len(X)):
            p = mx_ref.matmul(mx_ref.quantize(cut(w, len(X) * i + t)), X[t])
            z = p if t == 0 else z + p
        out.append(z)
    return out
def act(Z):
    return [np.maximum(z, 0) * C for z in Z]
def setup_inputs(rng):
    def f(*shape):
        return mx_ref.flush((rng.standard_normal(shape, dtype=np.float32) * np.exp2(rng.integers(-2, 3, shape[:-1] + (1,)))).astype(BF))
    return {"x": f(N, 128, 4 * NC), "w1": f(N, 128, G * 512), "w2": f(N, 128, 512)}
def setup_inputs_blocks(rng):
    d = setup_inputs(rng)
    for k in ("x", "w1", "w2"): d[k] = mx_ref.spread(d[k], rng, 4)
    return d
def setup_inputs_wide(rng):
    d = setup_inputs(rng)
    for k in ("x", "w1", "w2"): d[k] = mx_ref.flush((d[k].astype(np.float32) * np.exp2(rng.integers(-8, 9, (N, 1, 1))).astype(np.float32)).astype(BF))
    return d
def setup_inputs_zeros(rng):
    d = setup_inputs(rng); v = d["x"].reshape(N, 128, -1, 4).copy()
    v[np.broadcast_to((rng.random((N, 1, v.shape[2], 1)) < 0.33), v.shape)] = 0
    d["x"] = v.reshape(d["x"].shape)
    return d
def reference(x, w1, w2):
    h = [tile(act(layer(w1[j], [mx_ref.quantize(x[j])]))) for j in range(N)]
    y = np.zeros((N, 128, NC), np.float32)
    for r in range(N):
        t = np.concatenate([cut(h[j], r, 4 * M) for j in range(N)], axis=1)
        y[r] = mx_ref.matmul(mx_ref.quantize(w2[r]), mx_ref.quantize(t))
    return {"y": y}

from concourse.bass import DstId, RemoteDMATransfer
from concourse.mybir import dt, AluOpType, ActivationFunctionType

WORLD = 256
RUN, BLK, PIECE = 32, 64, 128
C = 0.047
K_HALF = 4
RSLOTS = 2
WIDE_FIRST = True

SCRATCH = {
    "xt": ("sbuf", [128, 1536], "bfloat16"),
    "w1t": ("sbuf", [128, 2048], "bfloat16"),
    "w2t": ("sbuf", [128, 512], "bfloat16"),
    "xq": ("sbuf", [128, 384], "float8_e4m3fn_x4"), "xs": ("sbuf", [128, 384], "uint8"),
    "w1q": ("sbuf", [128, 512], "float8_e4m3fn_x4"), "w1s": ("sbuf", [128, 512], "uint8"),
    "w2q": ("sbuf", [128, 128], "float8_e4m3fn_x4"), "w2s": ("sbuf", [128, 128], "uint8"),
    "ht": ("sbuf", [128, 1536], "bfloat16"),
    "hq": ("sbuf", [128, 256], "float8_e4m3fn_x4"), "hs": ("sbuf", [128, 256], "uint8"),
    "bq": ("sbuf", [128, 512], "float8_e4m3fn_x4"), "bs": ("sbuf", [128, 512], "uint8"),
    "rq": ("sbuf", [128, BLK * RSLOTS], "float8_e4m3fn_x4"), "rs": ("sbuf", [128, BLK * RSLOTS], "uint8"),
    "ps": ("psum", [128, 4096], "float32"),
    "yt": ("sbuf", [128, 384], "float32"),
}
SEMAPHORES = (["lx%d" % p for p in range(3)] + ["lw%d" % i for i in range(4)] + ["lv"]
              + ["qx%d" % p for p in range(3)] + ["qw%d" % i for i in range(4)] + ["qv"]
              + ["mm%d_%d" % (p, b) for p in range(3) for b in range(4)]
              + ["act%d" % p for p in range(3)] + ["hq%d" % p for p in range(3)]
              + ["rc%d" % s for s in range(RSLOTS)] + ["rp%d" % s for s in range(RSLOTS)]
              + ["arr", "sent", "mmA", "mmB", "cpA", "cpB", "stA", "stB"])

_CACHE = {}


def _bits(m):
    return [e for e in range(m.bit_length()) if (m >> e) & 1]


def _share(pool, k):
    m = 1
    while k and m * 2 * k <= len(pool):
        m *= 2
    return [pool[i * m:(i + 1) * m] for i in range(k)]


def make_plan(cores, topo):
    n = len(cores)
    rank_of = {c: r for r, c in enumerate(cores)}

    def key(c):
        return (topo.host(c), topo.chip(c))
    chips = []
    for c in cores:
        if key(c) not in chips:
            chips.append(key(c))
    nch = len(chips)
    mem = [[r for r in range(n) if key(cores[r]) == k] for k in chips]
    assert all(m == [2 * i, 2 * i + 1] for i, m in enumerate(mem))
    chip_of = [r // 2 for r in range(n)]

    def can(h, B):
        return all(topo.may_write(h, cores[b]) for b in mem[B])
    slots = {}
    route = {}

    def give(a, B, h):
        slots.setdefault(h, []).append((a, B))
        route[(a, B)] = (h, len(slots[h]) - 1)

    for a in range(n):
        ca = cores[a]
        for B in range(nch):
            b0 = cores[mem[B][0]]
            if B == chip_of[a] or topo.same_plane(ca, b0) or topo.mates(ca, b0):
                continue
            cand = [h for h in range(WORLD) if key(h) not in chips and h not in slots and topo.mates(h, b0)
                    and topo.same_plane(ca, h) and topo.may_write(ca, h) and can(h, B)]
            if cand:
                def busy(h):
                    return sum(1 for o in slots if key(o) == key(h) and topo.die(o) == topo.die(h))
                give(a, B, min(cand, key=lambda h: (busy(h), h)))
    for A in range(nch):
        load, rest = {}, []
        for a in mem[A]:
            ca = cores[a]
            todo = [B for B in range(nch) if B != A and (a, B) not in route]
            budget = K_HALF - (nch - 1 - len(todo))
            cand = [B for B in todo if can(ca, B)]
            cand.sort(key=lambda B: (topo.same_plane(ca, cores[mem[B][0]]), not topo.mates(ca, cores[mem[B][0]]), (B - A) % nch))
            for B in cand:
                if budget >= 2:
                    budget -= 2
                    route[(a, B)] = None
                    k = (topo.same_plane(ca, cores[mem[B][0]]), topo.die(ca))
                    load[k] = load.get(k, 0) + 1
            rest += [(a, B) for B in todo if (a, B) not in route]
        rest.sort(key=lambda u: (topo.same_plane(cores[u[0]], cores[mem[u[1]][0]]), u))
        helpers = [h for h in range(WORLD) if key(h) == chips[A] and h not in rank_of]
        for a, B in rest:
            cls = topo.same_plane(cores[a], cores[mem[B][0]])
            cand = [h for h in helpers if h not in slots and can(h, B)]
            if not cand and can(cores[a], B):
                route[(a, B)] = None
                continue
            if not cand:
                cand = [h for h in helpers if can(h, B) and len(slots[h]) < RSLOTS]
            h = min(cand, key=lambda h: (len(slots.get(h, [])), load.get((cls, topo.die(h)), 0), h))
            load[(cls, topo.die(h))] = load.get((cls, topo.die(h)), 0) + 1
            give(a, B, h)

    pieces, own_piece, sib_w = [], [], []
    for a in range(n):
        A = chip_of[a]
        rel = [B for B in range(nch) if B != A and route[(a, B)] is not None]
        rel.sort(key=lambda B: (key(route[(a, B)][0]) == chips[A], topo.same_plane(cores[a], cores[mem[B][0]]), B))
        d = [B for B in range(nch) if B != A and route[(a, B)] is None]
        seq = rel + [A] + d if len(rel) % 2 else rel + d + [A]
        pc = [seq[2 * p:2 * p + 2] for p in range(3)]
        op = [p for p in range(3) if A in pc[p]][0]
        other = [B for B in pc[op] if B != A][0]
        pc[op] = [A, other] if a == mem[A][0] else [other, A]
        pieces.append(pc)
        own_piece.append(op)
        sib_w.append(BLK if route[(a, other)] is not None else RUN)

    seg, use, ncol = [], [], []
    for r in range(n):
        first = r == mem[chip_of[r]][0]
        s, u, c = {}, {}, 0
        for j in range(n):
            s[j] = c
            if j == r:
                u[j] = c + (0 if first else PIECE - RUN)
                c += PIECE
            elif chip_of[j] == chip_of[r] and sib_w[j] == BLK:
                u[j] = c + (0 if first else RUN)
                c += BLK
            else:
                u[j] = c
                c += RUN
        seg.append(s)
        use.append(u)
        ncol.append(c)

    raw = {}
    for a in range(n):
        A, lst = chip_of[a], []
        nslot = 0
        for p in range(3):
            if p == own_piece[a]:
                buf, base = "b", seg[a][a]
            else:
                buf, base = "h", PIECE * nslot
                nslot += 1
            tr = []
            for i, B in enumerate(pieces[a][p]):
                o = base + BLK * i
                if B == A:
                    s = [r for r in mem[A] if r != a][0]
                    if sib_w[a] == BLK:
                        tr.append((buf, o, o + BLK, cores[s], "b", seg[s][a], "arr"))
                    else:
                        k = mem[A].index(s)
                        tr.append((buf, o + RUN * k, o + RUN * k + RUN, cores[s], "b", seg[s][a], "arr"))
                elif route[(a, B)] is not None:
                    h, sl = route[(a, B)]
                    tr.append((buf, o, o + BLK, h, "r", BLK * sl, sl))
                else:
                    for k, b in enumerate(mem[B]):
                        tr.append((buf, o + RUN * k, o + RUN * k + RUN, cores[b], "b", seg[b][a], "arr"))
            for w in sorted({t[2] - t[1] for t in tr}, reverse=True):
                lst.append((p, [t for t in tr if t[2] - t[1] == w]))
        raw[cores[a]] = lst
    for h, held in slots.items():
        raw[h] = [(sl, [("r", BLK * sl + RUN * k, BLK * sl + RUN * k + RUN, cores[b], "b", seg[b][a], "arr")
                        for k, b in enumerate(mem[B])]) for sl, (a, B) in enumerate(held)]

    calls, expect = {}, {}
    for c, lst in raw.items():
        masks = [topo.mask(c, t[3]) for _, tr in lst for t in tr]
        both, any_ = masks[0], 0
        for m in masks:
            both &= m
            any_ |= m
        lo, hi = _bits(both), _bits(any_ & ~both)
        left = False
        out = []
        for when, tr in lst:
            off = [t for t in tr if topo.mask(c, t[3]) == both]
            on = [t for t in tr if topo.mask(c, t[3]) != both]
            pool = lo + hi if (WIDE_FIRST and not off and not left) else hi
            left = left or bool(off)
            eng = list(zip(off, _share(lo, len(off)))) + list(zip(on, _share(pool, len(on))))
            for kind in "cp":
                item = []
                for t, es in eng:
                    sem = t[6] if t[6] == "arr" else "r%s%d" % (kind, t[6])
                    item.append(t[:6] + (sem, sum(1 << e for e in es), len(es)))
                    expect[(t[3], sem)] = expect.get((t[3], sem), 0) + len(es)
                    expect[(c, "sent")] = expect.get((c, "sent"), 0) + len(es)
                out.append((when, kind, item))
        calls[c] = out
    return dict(pieces=pieces, own_piece=own_piece, seg=seg, use=use, ncol=ncol, calls=calls, expect=expect,
                slots=slots, route=route)


def _send(g, core, T, topo, kind, item):
    tr = []
    for sb, lo, hi, d, db, dlo, sem, mask, _ in item:
        rid, pid = topo.addr(d, core)
        if kind == "c":
            src = T[sb + "q"][:, lo:hi].bitcast(dt.uint8)
            dst = T[db + "q"][:, dlo:dlo + hi - lo].bitcast(dt.uint8)
        else:
            src = T[sb + "s"][:, lo:hi]
            dst = T[db + "s"][:, dlo:dlo + hi - lo]
        tr.append(RemoteDMATransfer(dst_ids=[DstId(rid=rid, pnc=pid)], dma_engine_mask=mask, remote_sem=T.sem[sem],
                                    src=src, dst=dst))
    g.remote_dma_fused(tr, local_sem=T.sem.sent)


def rank_program(g, core, T, topo):
    if "p" not in _CACHE:
        _CACHE["p"] = make_plan(list(T.cores), topo)
    P = _CACHE["p"]
    S = T.sem
    rank = T.rank_of(core)
    if rank is None:
        if core not in P["calls"]:
            return
        for sl, kind, item in P["calls"][core]:
            sem = "r%s%d" % (kind, sl)
            g.wait_ge(S[sem], P["expect"][(core, sem)])
            _send(g, core, T, topo, kind, item)
        g.wait_ge(S.sent, P["expect"][(core, "sent")])
        return

    pieces, op = P["pieces"][rank], P["own_piece"][rank]
    seg, use, ncol = P["seg"][rank], P["use"][rank], P["ncol"][rank]
    V, TE, SC, SY = g.vector, g.tensor, g.scalar, g.sync

    def load_x(p):
        for i, q in enumerate((SY, SC)):
            B = pieces[p][i]
            q.dma_start(T.xt[:, 512 * p + 256 * i:512 * p + 256 * i + 256], T.x[:, 256 * B:256 * B + 256]).then_inc(S["lx%d" % p], 16)
    load_x(0)
    for i in range(4):
        (SY, SC)[i % 2].dma_start(T.w1t[:, 512 * i:512 * i + 512], T.w1[:, 512 * i:512 * i + 512]).then_inc(S["lw%d" % i], 16)
    load_x(1)
    load_x(2)
    SY.dma_start(T.w2t[:], T.w2[:]).then_inc(S.lv, 16)

    where, ns = [], 0
    for p in range(3):
        if p == op:
            where.append((T.bq, T.bs, seg[rank]))
        else:
            where.append((T.hq, T.hs, PIECE * ns))
            ns += 1

    def quant_x(p):
        V.wait_ge(S["lx%d" % p], 32)
        V.quantize_mx(T.xq[:, 128 * p:128 * p + 128], T.xs[:, 128 * p:128 * p + 128], T.xt[:, 512 * p:512 * p + 512]).then_inc(S["qx%d" % p], 1)

    def quant_h(p):
        q, s, o = where[p]
        V.wait_ge(S["act%d" % p], 4)
        V.quantize_mx(q[:, o:o + PIECE], s[:, o:o + PIECE], T.ht[:, 512 * p:512 * p + 512]).then_inc(S["hq%d" % p], 1)

    def bank(p, b):
        return 512 * ((4 * p + b) % 8)

    def act(p, b, on_vector):
        out = T.ht[:, 512 * p + b:512 * p + 512:4]
        z = T.ps[:, bank(p, b):bank(p, b) + PIECE]
        if on_vector:
            V.wait_ge(S["mm%d_%d" % (p, b)], 1)
            V.tensor_scalar(out, z, 0.0, C, AluOpType.max, AluOpType.mult).then_inc(S["act%d" % p], 1)
        else:
            SC.wait_ge(S["mm%d_%d" % (p, b)], 1)
            SC.activation(out, z, ActivationFunctionType.Relu, scale=C).then_inc(S["act%d" % p], 1)

    for p in range(3):
        TE.wait_ge(S["qx%d" % p], 1)
        if p == 2:
            TE.wait_ge(S.act0, 4)
        for b in range(4):
            if p == 0:
                TE.wait_ge(S["qw%d" % b], 1)
            TE.matmul_mx(T.ps[:, bank(p, b):bank(p, b) + PIECE], T.w1q[:, 128 * b:128 * b + 128], T.w1s[:, 128 * b:128 * b + 128],
                         T.xq[:, 128 * p:128 * p + 128], T.xs[:, 128 * p:128 * p + 128], True, True).then_inc(S["mm%d_%d" % (p, b)], 1)
    cut_j = min((j for j in range(1, len(T.cores)) if seg[j] >= PIECE and ncol - seg[j] >= PIECE), key=lambda j: abs(2 * seg[j] - ncol))
    cut = seg[cut_j]
    bA, bB = bank(1, 0), bank(1, 1)
    TE.wait_ge(S.qv, 1)
    TE.wait_ge(S.act1, 4)
    TE.wait_ge(S["hq%d" % op], 1)
    TE.wait_ge(S.arr, P["expect"][(core, "arr")])
    TE.matmul_mx(T.ps[:, bA:bA + cut], T.w2q[:], T.w2s[:], T.bq[:, 0:cut], T.bs[:, 0:cut], True, True).then_inc(S.mmA, 1)
    TE.matmul_mx(T.ps[:, bB:bB + ncol - cut], T.w2q[:], T.w2s[:], T.bq[:, cut:ncol], T.bs[:, cut:ncol], True, True).then_inc(S.mmB, 1)

    quant_x(0)
    for i in range(4):
        V.wait_ge(S["lw%d" % i], 16)
        V.quantize_mx(T.w1q[:, 128 * i:128 * i + 128], T.w1s[:, 128 * i:128 * i + 128], T.w1t[:, 512 * i:512 * i + 512]).then_inc(S["qw%d" % i], 1)
    for b in range(4):
        act(0, b, False)
    quant_h(0)
    quant_x(1)
    quant_x(2)
    for p in (1, 2):
        for b in range(4):
            act(p, b, b >= 2)
        quant_h(p)
    V.wait_ge(S.lv, 16)
    V.quantize_mx(T.w2q[:], T.w2s[:], T.w2t[:]).then_inc(S.qv, 1)

    seen = -1
    for p, kind, item in P["calls"][core]:
        if p != seen:
            g.wait_ge(S["hq%d" % p], 1)
            seen = p
        _send(g, core, T, topo, kind, item)

    def runs(js, base, col0):
        out = []
        for j in js:
            if out and out[-1][0] + out[-1][2] == use[j]:
                out[-1][2] += RUN
            else:
                out.append([use[j], RUN * j, RUN])
        return [(base + u - col0, y, w) for u, y, w in out]
    ra = runs(range(cut_j), bA, 0)
    rb = runs(range(cut_j, len(T.cores)), bB, cut)
    V.wait_ge(S.mmA, 1)
    for u, y, w in ra:
        V.tensor_copy(T.yt[:, y:y + w], T.ps[:, u:u + w]).then_inc(S.cpA, 1)
    SC.wait_ge(S.mmB, 1)
    for u, y, w in rb:
        SC.activation(T.yt[:, y:y + w], T.ps[:, u:u + w], ActivationFunctionType.Copy).then_inc(S.cpB, 1)
    ya = RUN * cut_j
    SY.wait_ge(S.cpA, len(ra))
    SY.dma_start(T.y[:, 0:ya], T.yt[:, 0:ya]).then_inc(S.stA, 16)
    SC.wait_ge(S.cpB, len(rb))
    SC.dma_start(T.y[:, ya:], T.yt[:, ya:]).then_inc(S.stB, 16)
    SY.wait_ge(S.stA, 16)
    SC.wait_ge(S.stB, 16)
    g.wait_ge(S.sent, P["expect"][(core, "sent")])
